import numpy as np
import ml_dtypes


def mxq(x, axis, fmt="e4m3"):
    dtype, down = {"e4m3": (ml_dtypes.float8_e4m3fn, 7), "e5m2": (ml_dtypes.float8_e5m2, 14)}[fmt]
    v = np.moveaxis(np.asarray(x, np.float32).astype(ml_dtypes.bfloat16).astype(np.float64), axis, -1)
    blocks = v.reshape(v.shape[:-1] + (-1, 32))
    amax = np.abs(blocks).max(-1, keepdims=True)
    byte = np.maximum(np.where(amax > 0, np.frexp(amax)[1] - 1 + 127, 0) - down, 1)
    scale = np.exp2(byte - 127.0)
    codes = (blocks / scale).astype(np.float32).astype(dtype).astype(np.float64)
    return np.moveaxis((codes * scale).reshape(v.shape), -1, axis)


WIDE = False


def mx_kscale(k):
    if not WIDE:
        return np.ones(k)
    levels = np.array([10, -10, 5, -5, 0])
    if k % 512:
        return np.exp2(np.random.permutation(np.resize(levels, k // 32))).repeat(32)
    a = np.empty((k // 512, 16))
    for p in range(k // 512):
        a[p, :8] = np.random.permutation(np.resize(levels, 8))
        for g in range(8):
            far = levels[np.abs(levels - a[p, g]) >= 10]
            a[p, g + 8] = far[np.random.randint(len(far))]
    return np.exp2(a.ravel()).repeat(32)


def f64(x):
    return np.asarray(x).astype(np.float64)


def striped(idx):
    return np.tile(idx.reshape(-1, 16).T, (8, 1)).astype(np.uint16)


def unstriped(offs):
    return offs[:16].T.reshape(-1).astype(np.int64)


E2M1 = np.array([0.0, 0.5, 1.0, 1.5, 2.0, 3.0, 4.0, 6.0, -0.0, -0.5, -1.0, -1.5, -2.0, -3.0, -4.0, -6.0])


def pack_weight(w, fmt):
    k, n = w.shape
    w = f64(np.asarray(w, np.float32).astype(ml_dtypes.bfloat16)).reshape(k // 32, 32, n)
    amax = np.abs(w).max(1)
    if fmt == "e4m3":
        byte = np.frexp(amax)[1] - 1 + 127 - 7
    else:
        mant, ex = np.frexp(amax / 6.0)
        byte = np.where(mant > 0.5, ex, ex - 1) + 127
    byte = np.clip(np.where(amax > 0, byte, 1), 1, 254)
    scaled = (w * np.exp2(127.0 - byte)[:, None, :]).reshape(k, n).astype(np.float32)
    by_word = np.ascontiguousarray(scaled.reshape(k // 512, 128, 4, n).transpose(0, 1, 3, 2))
    if fmt == "e4m3":
        words = by_word.astype(ml_dtypes.float8_e4m3fn).view(np.uint8)
    else:
        c = by_word.astype(ml_dtypes.float4_e2m1fn).view(np.uint8) & 0xF
        words = (c[..., 0::2] | (c[..., 1::2] << 4)).reshape(k // 512, 128, 2 * n)
    return np.ascontiguousarray(words), np.ascontiguousarray(byte.astype(np.uint8).reshape(k // 512, 16, n))


def unpack_weight(words, scales, fmt):
    g, _, n = scales.shape
    words = np.ascontiguousarray(words).reshape(g, 128, n, -1)
    if fmt == "e4m3":
        vals = words.view(ml_dtypes.float8_e4m3fn).astype(np.float64)
    else:
        nib = np.empty((g, 128, n, 4), np.uint8)
        nib[..., 0::2] = words & 0xF
        nib[..., 1::2] = words >> 4
        vals = E2M1[nib]
    vals = vals * np.repeat(np.exp2(scales.astype(np.float64) - 127.0), 8, axis=1)[..., None]
    return vals.transpose(0, 1, 3, 2).reshape(g * 512, n)


def gelu(v):
    return 0.5 * v * (1.0 + np.tanh(np.sqrt(2.0 / np.pi) * (v + 0.044715 * v**3)))


def striped8(idx):
    return np.concatenate([v.reshape(-1, 16).T for v in idx]).astype(np.uint16)


def unstriped8(offs):
    return np.stack([offs[16 * g:16 * g + 16].T.reshape(-1) for g in range(8)]).astype(np.int64)


def heads(h, wgt, idx8):
    r = np.arange(h.shape[0])
    return wgt[r // 4 % 128] * h[r[:, None], idx8[r % 512 // 64]]


def bf(x):
    return np.asarray(x, np.float32).astype(ml_dtypes.bfloat16)


def planes(Y):
    n, m = Y.shape
    b = f64(bf(Y)).reshape(n // 32, 32, m)
    amax = np.abs(b).max(1)
    byte = np.clip(np.where(amax > 0, np.frexp(amax)[1] - 1 + 127 - 7, 1), 1, 254)
    codes = (b * np.exp2(127.0 - byte)[:, None, :]).reshape(n, m).astype(np.float32).astype(ml_dtypes.float8_e4m3fn).view(np.uint8)
    words = codes.reshape(n // 512, 128, 4, m).transpose(0, 1, 3, 2)
    return np.ascontiguousarray(words), np.ascontiguousarray(byte.astype(np.uint8).reshape(n // 512, 16, m))


K, H, T, S, P = 1024, 1024, 4096, 1024, 512

def setup_inputs():
    n = np.random.standard_normal
    s, u = mx_kscale(K)[:, None], mx_kscale(H)[:, None]
    size = np.exp(0.8 * n(H))
    tab_words, tab_scales = pack_weight(n((K, T)) * s, "e4m3")
    w1_words, w1_scales = pack_weight(n((K, H)) / np.sqrt(K) / s * u.T, "e2m1")
    return {
        "tab_words": tab_words, "tab_scales": tab_scales,
        "offs": striped(np.random.permutation(T)[:S]),
        "w1_words": w1_words, "w1_scales": w1_scales,
        "b1": (0.5 * n(H) * u[:, 0]).astype(np.float32),
        "offs2": striped8(np.stack([np.random.permutation(S)[:P] for _ in range(8)])),
        "offs3": striped8(np.stack([np.random.permutation(S)[:P] for _ in range(8)])),
        "wga": np.repeat(np.random.uniform(0.5, 2.0, (8, P)), 16, axis=0).astype(np.float32),
        "wgb": np.repeat(np.random.uniform(0.5, 2.0, (8, P)), 16, axis=0).astype(np.float32),
        "d": (0.5 * n(H) * u[:, 0]).astype(np.float32),
        "w2": (n((H, H)) / np.sqrt(H) / u * size).astype(np.float32),
        "b2": (0.5 * n(H) * size).astype(np.float32),
        "rs": (0.8 * size / u[:, 0]).astype(np.float32),
    }

def reference(tab_words, tab_scales, offs, w1_words, w1_scales, b1, offs2, offs3, wga, wgb, d, w2, b2, rs):
    v = unpack_weight(tab_words, tab_scales, "e4m3")[:, unstriped(offs)]
    w1 = unpack_weight(w1_words, w1_scales, "e2m1")
    h = (w1.T @ v) + f64(b1)[:, None]
    xa = heads(h, f64(wga), unstriped8(offs2))
    xb = heads(h, f64(wgb), unstriped8(offs3))
    z = np.maximum(xa, xb + f64(d)[:, None])
    y = mxq(f64(w2), 0, "e4m3").T @ mxq(z, 0, "e4m3")
    y = y + f64(b2)[:, None] + f64(rs)[:, None] * xa
    words, scales = planes(y)
    return y, words, scales

@@ -1,0 +1,299 @@
+from contextlib import ExitStack
+
+import concourse.mybir as mybir
+
+K, H, T, S, J = 1024, 1024, 4096, 1024, 512
+FLOPS = 2 * K * H * S + 2 * H * H * J
+
+F32 = mybir.dt.float32
+BF16 = mybir.dt.bfloat16
+I32 = mybir.dt.int32
+U32 = mybir.dt.uint32
+U16 = mybir.dt.uint16
+U8 = mybir.dt.uint8
+FP8X4 = mybir.dt.float8_e4m3fn_x4
+FP4X4 = mybir.dt.float4_e2m1fn_x4
+MULT = mybir.AluOpType.mult
+ADD = mybir.AluOpType.add
+MAX = mybir.AluOpType.max
+IDENTITY = mybir.ActivationFunctionType.Identity
+
+P = 128
+BANK = 512
+CHUNKS = ((0, 256), (256, 128), (384, 128))
+
+
+def tile_list_salmon_origin_features_kernel(
+    tc, tab_words, tab_scales, offs, w1_words, w1_scales, b1, offs2, offs3, wga, wgb, d, w2, b2, rs,
+    out_0, out_1, out_2,
+):
+    nc = tc.nc
+    with ExitStack() as ctx:
+        lists = ctx.enter_context(tc.tile_pool(name="lists", bufs=1))
+        sb = ctx.enter_context(tc.tile_pool(name="sb", bufs=1))
+        ring = ctx.enter_context(tc.tile_pool(name="ring", bufs=3))
+        psum = ctx.enter_context(tc.psum_pool(name="psum", bufs=8))
+
+        def tile(shape, dtype, name, tag=None):
+            return sb.tile(shape, dtype, name=name, tag=tag or name, align_bytes=64)
+
+        idx = lists.tile([P, S // 16], U16, name="idx")
+        idx2 = lists.tile([P, J // 16], U16, name="idx2")
+        idx3 = lists.tile([P, J // 16], U16, name="idx3")
+        tab_sc = tile([P, T], U8, "tab_sc")
+        w1_sc_raw = tile([P, 2 * H], U8, "w1_sc_raw")
+        v_sc = [tile([P, S], U8, "v_sc%d" % a) for a in range(2)]
+        nc.vector.memset(w1_sc_raw[:].bitcast(I32), 0)
+        nc.vector.memset(tab_sc[32:64, :].bitcast(I32), 0)
+        nc.vector.memset(tab_sc[64:128, :].bitcast(I32), 0)
+        for a in range(2):
+            nc.vector.memset(v_sc[a][:].bitcast(I32), 0)
+
+        w1_raw = tile([P, 2, 2 * H], U8, "w1_raw")
+        tab = [tile([P, T], I32, "tab%d" % a) for a in range(2)]
+        wa = tile([P, J], F32, "wa")
+        wb = tile([P, J], F32, "wb")
+
+        def load_table(a):
+            nc.sync.dma_start(out=tab[a][:], in_=tab_words[a].rearrange("p t i -> p (t i)").bitcast(I32))
+
+        nc.sync.dma_start(idx[:], offs)
+        nc.sync.dma_start(
+            out=tab_sc[0:32, :].bitcast(I32), in_=tab_scales.rearrange("a q t -> (a q) t").bitcast(I32)
+        )
+        nc.sync.dma_start(out=w1_raw[:].bitcast(I32), in_=w1_words.rearrange("a p c -> p a c").bitcast(I32))
+        load_table(0)
+        nc.sync.dma_start(idx2[:], offs2)
+        nc.sync.dma_start(idx3[:], offs3)
+        load_table(1)
+        nc.sync.dma_start(out=wa[:], in_=wga)
+        nc.sync.dma_start(out=wb[:], in_=wgb)
+        for q in range(4):
+            nc.gpsimd.dma_start(
+                out=w1_sc_raw[32 * q : 32 * q + 4, :].rearrange("r (a c) -> r a c", a=2).bitcast(I32),
+                in_=w1_scales[:, 4 * q : 4 * q + 4, :].rearrange("a r c -> r a c").bitcast(I32),
+            )
+
+        picked_sc = tile([P, S], U8, "picked_sc")
+        nc.vector.tensor_copy(picked_sc[:], tab_sc[:].indirect(idx[:]))
+        for a, queue in enumerate((nc.scalar, nc.gpsimd)):
+            for q in range(4):
+                queue.dma_start(
+                    out=v_sc[a][32 * q : 32 * q + 4, :].bitcast(I32),
+                    in_=picked_sc[16 * a + 4 * q : 16 * a + 4 * q + 4, :].bitcast(I32),
+                )
+
+        rows = {}
+        for name, vec in (("b1", b1), ("d", d), ("b2", b2), ("rs", rs)):
+            rows[name] = tile([P, 2, 4], F32, name + "_rows")
+            nc.gpsimd.dma_start(out=rows[name][:], in_=vec.rearrange("(b p t) -> p b t", b=2, t=4))
+
+        w1_q = [tile([P, 2 * 2 * 512], U8, "w1_q%d" % b) for b in range(2)]
+        w1_sc = [tile([P, 2 * 512], U8, "w1_sc%d" % b) for b in range(2)]
+
+        def deal_w1(b):
+            words = w1_raw[:].bitcast(U16)[:, :, 512 * b : 512 * (b + 1)]
+            nc.vector.tensor_copy(
+                out=w1_q[b][:].bitcast(U16).rearrange("p (a t m) -> p a t m", a=2, t=4),
+                in_=words.rearrange("p a (m t) -> p a t m", t=4),
+            )
+            scales = w1_sc_raw[:].rearrange("p (a c) -> p a c", a=2)[:, :, 512 * b : 512 * (b + 1)]
+            nc.vector.tensor_copy(
+                out=w1_sc[b][:].rearrange("p (a t m) -> p a t m", a=2, t=4),
+                in_=scales.rearrange("p a (m t) -> p a t m", t=4),
+            )
+
+        deal_w1(0)
+        v_q = {}
+        v_all = tile([P, S], U32, "v_q0")
+        nc.vector.tensor_copy(v_all[:], tab[0][:].bitcast(U32).indirect(idx[:]))
+        for half in range(2):
+            v_q[0, half] = v_all[:, BANK * half : BANK * (half + 1)]
+            v_half = tile([P, BANK], U32, "v_q1%d" % half)
+            nc.vector.tensor_copy(
+                v_half[:], tab[1][:].bitcast(U32).indirect(idx[:, 32 * half : 32 * (half + 1)])
+            )
+            v_q[1, half] = v_half[:]
+        deal_w1(1)
+
+        w2_raw = [tile([P, 4, H], F32, "w2_raw%d" % b, tag="tab%d" % b) for b in range(2)]
+        for b in range(2):
+            nc.sync.dma_start(
+                out=w2_raw[b][:], in_=w2[512 * b : 512 * (b + 1), :].rearrange("(p j) n -> p j n", j=4)
+            )
+
+        h = {}
+        for b in range(2):
+            for t in range(4):
+                h[b, t] = tile([P, S], F32, "h%d%d" % (b, t))
+                for half in range(2):
+                    acc = psum.tile([P, BANK], F32, name="acc", tag="bank")
+                    for a in range(2):
+                        col = 512 * a + P * t
+                        nc.tensor.matmul_mx(
+                            out=acc[:],
+                            lhsT=w1_q[b][:, 2 * col : 2 * (col + P)].bitcast(FP4X4),
+                            lhsT_scale=w1_sc[b][:, col : col + P],
+                            rhs=v_q[a, half].bitcast(FP8X4),
+                            rhs_scale=v_sc[a][:, BANK * half : BANK * (half + 1)],
+                            start=(a == 0),
+                            stop=(a == 1),
+                        )
+                    nc.scalar.activation(
+                        out=h[b, t][:, BANK * half : BANK * (half + 1)], in_=acc[:], func=IDENTITY,
+                        bias=rows["b1"][:, b, t : t + 1],
+                    )
+
+        y_sc = tile([P, 2, J], U8, "y_sc")
+        w2_bf, w2_q, w2_sc = {}, {}, {}
+        z, z_bf, z_q, z_sc = {}, {}, {}, {}
+        side, y, y_bf, y_q, banks = {}, {}, {}, {}, {}
+        chain = ["xb"]
+
+        def round_w2(b, g):
+            w2_bf[b, g] = tile([P, 4 * 512], BF16, "w2_bf%d%d" % (b, g))
+            nc.scalar.copy(
+                out=w2_bf[b, g][:].rearrange("p (t m j) -> p m t j", t=4, j=4),
+                in_=w2_raw[b][:, :, 512 * g : 512 * (g + 1)].rearrange("p j (m t) -> p m t j", t=4),
+            )
+
+        def quantize_w2(b, g):
+            w2_q[b, g] = tile([P, 512], U32, "w2_q%d%d" % (b, g))
+            w2_sc[b, g] = tile([P, 512], U8, "w2_sc%d%d" % (b, g))
+            nc.vector.quantize_mx(out=w2_q[b, g][:].bitcast(FP8X4), scales=w2_sc[b, g][:], in_=w2_bf[b, g][:])
+            chain[0] = "w2_bf%d%d" % (b, g)
+
+        def interleave(dst, src):
+            nc.scalar.copy(
+                out=dst.rearrange("p (c i t) -> p c t i", i=4, t=4),
+                in_=src.rearrange("p t (c i) -> p c t i", i=4),
+            )
+
+        def pick(b, t, j0, w):
+            if t == 0:
+                z[b, j0] = tile([P, 4, w], BF16, "z%d_%d" % (b, j0))
+                side[b, j0] = tile([P, 4, w], F32, "side%d_%d" % (b, j0))
+            cols = slice(j0 // 16, (j0 + w) // 16)
+            xa = ring.tile([P, w], F32, name="xa", tag="xa")
+            xb = tile([P, w], F32, "xb", tag=chain[0])
+            nc.vector.tensor_tensor(xa[:], h[b, t][:].indirect(idx2[:, cols]), wa[:, j0 : j0 + w], MULT)
+            nc.vector.tensor_tensor(xb[:], h[b, t][:].indirect(idx3[:, cols]), wb[:, j0 : j0 + w], MULT)
+            nc.vector.scalar_tensor_tensor(
+                out=z[b, j0][:, t, :], in0=xb[:], scalar=rows["d"][:, b, t : t + 1], in1=xa[:], op0=ADD, op1=MAX
+            )
+            nc.scalar.activation(
+                out=side[b, j0][:, t, :], in_=xa[:], func=IDENTITY,
+                scale=rows["rs"][:, b, t : t + 1], bias=rows["b2"][:, b, t : t + 1],
+            )
+
+        def weave_z(b, j0, w):
+            z_bf[b, j0] = tile([P, 4 * w], BF16, "z_bf%d_%d" % (b, j0))
+            interleave(z_bf[b, j0][:], z[b, j0][:])
+
+        def quantize_z(b, j0, w):
+            z_q[b, j0] = tile([P, w], U32, "z_q%d_%d" % (b, j0))
+            z_sc[b, j0] = tile([P, w], U8, "z_sc%d_%d" % (b, j0))
+            nc.vector.quantize_mx(out=z_q[b, j0][:].bitcast(FP8X4), scales=z_sc[b, j0][:], in_=z_bf[b, j0][:])
+            chain[0] = "z_bf%d_%d" % (b, j0)
+
+        def product(b, j0, w):
+            per_bank = BANK // w
+            z0 = 0 if b == 0 else j0
+            for g in range(2):
+                for t in range(4):
+                    key = (j0, g, t // per_bank)
+                    slot = t % per_bank
+                    if b == 0 and slot == 0:
+                        banks[key] = psum.tile([P, BANK], F32, name="acc", tag="bank")
+                    nc.tensor.matmul_mx(
+                        out=banks[key][:, slot * w : (slot + 1) * w],
+                        lhsT=w2_q[b, g][:, P * t : P * (t + 1)].bitcast(FP8X4),
+                        lhsT_scale=w2_sc[b, g][:, P * t : P * (t + 1)],
+                        rhs=z_q[b, z0][:, j0 - z0 : j0 - z0 + w].bitcast(FP8X4),
+                        rhs_scale=z_sc[b, z0][:, j0 - z0 : j0 - z0 + w],
+                        start=(b == 0 and slot == 0),
+                        stop=(b == 1 and slot == per_bank - 1),
+                    )
+
+        def finish(g, j0, w):
+            per_bank = BANK // w
+            z0 = 0 if g == 0 else j0
+            y[g, j0] = tile([P, 4, w], F32, "y%d_%d" % (g, j0))
+            for n in range(4 // per_bank):
+                ts = slice(n * per_bank, (n + 1) * per_bank)
+                nc.vector.tensor_tensor(
+                    y[g, j0][:, ts, :],
+                    banks[j0, g, n][:].rearrange("p (t j) -> p t j", j=w),
+                    side[g, z0][:, ts, j0 - z0 : j0 - z0 + w],
+                    ADD,
+                )
+            nc.sync.dma_start(
+                out=out_0[512 * g : 512 * (g + 1), j0 : j0 + w].rearrange("(p t) j -> p t j", t=4),
+                in_=y[g, j0][:],
+            )
+            y_bf[g, j0] = tile([P, 4 * w], BF16, "y_bf%d_%d" % (g, j0))
+            interleave(y_bf[g, j0][:], y[g, j0][:])
+            if g == 1:
+                chain[0] = "side1_%d" % j0
+
+        def quantize_y(j0, w):
+            y_q[j0] = tile([P, 2, w], I32, "y_q%d" % j0)
+            for g in range(2):
+                nc.vector.quantize_mx(
+                    out=y_q[j0][:, g, :].bitcast(FP8X4), scales=y_sc[:, g, j0 : j0 + w], in_=y_bf[g, j0][:]
+                )
+            nc.sync.dma_start(
+                out=out_1.rearrange("g p m t -> p g (m t)")[:, :, 4 * j0 : 4 * (j0 + w)].bitcast(I32),
+                in_=y_q[j0][:],
+            )
+
+        first, second, third = CHUNKS
+        for t in range(4):
+            pick(0, t, 0, J)
+            if t >= 2:
+                round_w2(0, t - 2)
+        weave_z(0, 0, J)
+        round_w2(1, 0)
+        pick(1, 0, *first)
+        quantize_w2(0, 0)
+        quantize_w2(0, 1)
+        pick(1, 1, *first)
+        pick(1, 2, *first)
+        quantize_z(0, 0, J)
+        for chunk in CHUNKS:
+            product(0, *chunk)
+        round_w2(1, 1)
+        pick(1, 3, *first)
+        weave_z(1, *first)
+        quantize_w2(1, 0)
+        pick(1, 0, *second)
+        quantize_w2(1, 1)
+        pick(1, 1, *second)
+        quantize_z(1, *first)
+        product(1, *first)
+        pick(1, 2, *second)
+        pick(1, 3, *second)
+        weave_z(1, *second)
+        finish(0, *first)
+        pick(1, 0, *third)
+        quantize_z(1, *second)
+        product(1, *second)
+        finish(1, *first)
+        for t in range(1, 4):
+            pick(1, t, *third)
+        weave_z(1, *third)
+        finish(0, *second)
+        finish(1, *second)
+        quantize_z(1, *third)
+        product(1, *third)
+        quantize_y(*first)
+        finish(0, *third)
+        finish(1, *third)
+        quantize_y(*second)
+        quantize_y(*third)
+        for q in range(4):
+            queue = nc.sync if q % 2 == 0 else nc.scalar
+            queue.dma_start(
+                out=out_2[:, 4 * q : 4 * q + 4, :].rearrange("g r m -> r g m").bitcast(I32),
+                in_=y_sc[32 * q : 32 * q + 4, :, :].bitcast(I32),
+            )

@@ -31,6 +31,7 @@ def tile_list_salmon_origin_features_kernel(
     with ExitStack() as ctx:
         lists = ctx.enter_context(tc.tile_pool(name="lists", bufs=1))
         sb = ctx.enter_context(tc.tile_pool(name="sb", bufs=1))
+        shared = ctx.enter_context(tc.tile_pool(name="shared", bufs=1))
         ring = ctx.enter_context(tc.tile_pool(name="ring", bufs=3))
         psum = ctx.enter_context(tc.psum_pool(name="psum", bufs=8))
 
@@ -40,7 +41,7 @@ def tile_list_salmon_origin_features_kernel(
         idx = lists.tile([P, S // 16], U16, name="idx")
         idx2 = lists.tile([P, J // 16], U16, name="idx2")
         idx3 = lists.tile([P, J // 16], U16, name="idx3")
-        tab_sc = tile([P, T], U8, "tab_sc")
+        tab_sc = shared.tile([P, T], U8, name="tab_sc", offset=1024)
         w1_sc_raw = tile([P, 2 * H], U8, "w1_sc_raw")
         v_sc = [tile([P, S], U8, "v_sc%d" % a) for a in range(2)]
         nc.vector.memset(w1_sc_raw[:].bitcast(I32), 0)
@@ -50,9 +51,7 @@ def tile_list_salmon_origin_features_kernel(
             nc.vector.memset(v_sc[a][:].bitcast(I32), 0)
 
         w1_raw = tile([P, 2, 2 * H], U8, "w1_raw")
-        tab = [tile([P, T], I32, "tab%d" % a) for a in range(2)]
-        wa = tile([P, J], F32, "wa")
-        wb = tile([P, J], F32, "wb")
+        tab = [tile([P, T], I32, "tab0")]
 
         def load_table(a):
             nc.sync.dma_start(out=tab[a][:], in_=tab_words[a].rearrange("p t i -> p (t i)").bitcast(I32))
@@ -62,26 +61,31 @@ def tile_list_salmon_origin_features_kernel(
             out=tab_sc[0:32, :].bitcast(I32), in_=tab_scales.rearrange("a q t -> (a q) t").bitcast(I32)
         )
         nc.sync.dma_start(out=w1_raw[:].bitcast(I32), in_=w1_words.rearrange("a p c -> p a c").bitcast(I32))
-        load_table(0)
         nc.sync.dma_start(idx2[:], offs2)
         nc.sync.dma_start(idx3[:], offs3)
-        load_table(1)
-        nc.sync.dma_start(out=wa[:], in_=wga)
-        nc.sync.dma_start(out=wb[:], in_=wgb)
+        load_table(0)
         for q in range(4):
-            nc.gpsimd.dma_start(
+            nc.scalar.dma_start(
                 out=w1_sc_raw[32 * q : 32 * q + 4, :].rearrange("r (a c) -> r a c", a=2).bitcast(I32),
                 in_=w1_scales[:, 4 * q : 4 * q + 4, :].rearrange("a r c -> r a c").bitcast(I32),
             )
 
         picked_sc = tile([P, S], U8, "picked_sc")
         nc.vector.tensor_copy(picked_sc[:], tab_sc[:].indirect(idx[:]))
-        for a, queue in enumerate((nc.scalar, nc.gpsimd)):
+        for a in range(2):
             for q in range(4):
-                queue.dma_start(
+                if (a, q) == (0, 1):
+                    tab.append(shared.tile([P, T], I32, name="tab1", offset=4096))
+                    load_table(1)
+                nc.sync.dma_start(
                     out=v_sc[a][32 * q : 32 * q + 4, :].bitcast(I32),
                     in_=picked_sc[16 * a + 4 * q : 16 * a + 4 * q + 4, :].bitcast(I32),
                 )
+
+        wa = shared.tile([P, J], F32, name="wa", offset=0)
+        wb = shared.tile([P, J], F32, name="wb", offset=2048)
+        nc.sync.dma_start(out=wa[:], in_=wga)
+        nc.sync.dma_start(out=wb[:], in_=wgb)
 
         rows = {}
         for name, vec in (("b1", b1), ("d", d), ("b2", b2), ("rs", rs)):
@@ -116,7 +120,10 @@ def tile_list_salmon_origin_features_kernel(
             v_q[1, half] = v_half[:]
         deal_w1(1)
 
-        w2_raw = [tile([P, 4, H], F32, "w2_raw%d" % b, tag="tab%d" % b) for b in range(2)]
+        w2_raw = [
+            tile([P, 4, H], F32, "w2_raw0", tag="tab0"),
+            shared.tile([P, 4, H], F32, name="w2_raw1", offset=4096),
+        ]
         for b in range(2):
             nc.sync.dma_start(
                 out=w2_raw[b][:], in_=w2[512 * b : 512 * (b + 1), :].rearrange("(p j) n -> p j n", j=4)

@@ -20,6 +20,7 @@ IDENTITY = mybir.ActivationFunctionType.Identity
 
 P = 128
 BANK = 512
+LATE = 384
 CHUNKS = ((0, 256), (256, 128), (384, 128))
 
 
@@ -32,8 +33,8 @@ def tile_list_salmon_origin_features_kernel(
         lists = ctx.enter_context(tc.tile_pool(name="lists", bufs=1))
         sb = ctx.enter_context(tc.tile_pool(name="sb", bufs=1))
         shared = ctx.enter_context(tc.tile_pool(name="shared", bufs=1))
-        ring = ctx.enter_context(tc.tile_pool(name="ring", bufs=3))
-        psum = ctx.enter_context(tc.psum_pool(name="psum", bufs=8))
+        ring = ctx.enter_context(tc.tile_pool(name="ring", bufs=5))
+        psum = ctx.enter_context(tc.psum_pool(name="psum", bufs=1))
 
         def tile(shape, dtype, name, tag=None):
             return sb.tile(shape, dtype, name=name, tag=tag or name, align_bytes=64)
@@ -134,7 +135,7 @@ def tile_list_salmon_origin_features_kernel(
             for t in range(4):
                 h[b, t] = tile([P, S], F32, "h%d%d" % (b, t))
                 for half in range(2):
-                    acc = psum.tile([P, BANK], F32, name="acc", tag="bank")
+                    acc = psum.tile([P, BANK], F32, name="acc", tag="bank%d" % ((2 * (4 * b + t) + half) % 3))
                     for a in range(2):
                         col = 512 * a + P * t
                         nc.tensor.matmul_mx(
@@ -170,8 +171,8 @@ def tile_list_salmon_origin_features_kernel(
             nc.vector.quantize_mx(out=w2_q[b, g][:].bitcast(FP8X4), scales=w2_sc[b, g][:], in_=w2_bf[b, g][:])
             chain[0] = "w2_bf%d%d" % (b, g)
 
-        def interleave(dst, src):
-            nc.scalar.copy(
+        def interleave(copy, dst, src):
+            copy(
                 out=dst.rearrange("p (c i t) -> p c t i", i=4, t=4),
                 in_=src.rearrange("p t (c i) -> p c t i", i=4),
             )
@@ -195,7 +196,7 @@ def tile_list_salmon_origin_features_kernel(
 
         def weave_z(b, j0, w):
             z_bf[b, j0] = tile([P, 4 * w], BF16, "z_bf%d_%d" % (b, j0))
-            interleave(z_bf[b, j0][:], z[b, j0][:])
+            interleave(nc.scalar.copy, z_bf[b, j0][:], z[b, j0][:])
 
         def quantize_z(b, j0, w):
             z_q[b, j0] = tile([P, w], U32, "z_q%d_%d" % (b, j0))
@@ -203,15 +204,15 @@ def tile_list_salmon_origin_features_kernel(
             nc.vector.quantize_mx(out=z_q[b, j0][:].bitcast(FP8X4), scales=z_sc[b, j0][:], in_=z_bf[b, j0][:])
             chain[0] = "z_bf%d_%d" % (b, j0)
 
-        def product(b, j0, w):
-            per_bank = BANK // w
-            z0 = 0 if b == 0 else j0
-            for g in range(2):
+        def product(b, g, chunks):
+            for j0, w in chunks:
+                per_bank = BANK // w
+                z0 = 0 if b == 0 or j0 < LATE else LATE
                 for t in range(4):
                     key = (j0, g, t // per_bank)
                     slot = t % per_bank
                     if b == 0 and slot == 0:
-                        banks[key] = psum.tile([P, BANK], F32, name="acc", tag="bank")
+                        banks[key] = psum.tile([P, BANK], F32, name="acc", tag="bank%d" % len(banks))
                     nc.tensor.matmul_mx(
                         out=banks[key][:, slot * w : (slot + 1) * w],
                         lhsT=w2_q[b, g][:, P * t : P * (t + 1)].bitcast(FP8X4),
@@ -222,9 +223,9 @@ def tile_list_salmon_origin_features_kernel(
                         stop=(b == 1 and slot == per_bank - 1),
                     )
 
-        def finish(g, j0, w):
+        def finish(copy, g, j0, w):
             per_bank = BANK // w
-            z0 = 0 if g == 0 else j0
+            z0 = 0 if g == 0 or j0 < LATE else LATE
             y[g, j0] = tile([P, 4, w], F32, "y%d_%d" % (g, j0))
             for n in range(4 // per_bank):
                 ts = slice(n * per_bank, (n + 1) * per_bank)
@@ -239,9 +240,7 @@ def tile_list_salmon_origin_features_kernel(
                 in_=y[g, j0][:],
             )
             y_bf[g, j0] = tile([P, 4 * w], BF16, "y_bf%d_%d" % (g, j0))
-            interleave(y_bf[g, j0][:], y[g, j0][:])
-            if g == 1:
-                chain[0] = "side1_%d" % j0
+            interleave(copy, y_bf[g, j0][:], y[g, j0][:])
 
         def quantize_y(j0, w):
             y_q[j0] = tile([P, 2, w], I32, "y_q%d" % j0)
@@ -255,47 +254,44 @@ def tile_list_salmon_origin_features_kernel(
             )
 
         first, second, third = CHUNKS
-        for t in range(4):
+        for t in range(3):
             pick(0, t, 0, J)
-            if t >= 2:
-                round_w2(0, t - 2)
+        round_w2(0, 0)
+        pick(0, 3, 0, J)
         weave_z(0, 0, J)
         round_w2(1, 0)
-        pick(1, 0, *first)
+        pick(1, 0, 0, LATE)
         quantize_w2(0, 0)
-        quantize_w2(0, 1)
-        pick(1, 1, *first)
-        pick(1, 2, *first)
+        pick(1, 1, 0, LATE)
+        round_w2(0, 1)
         quantize_z(0, 0, J)
-        for chunk in CHUNKS:
-            product(0, *chunk)
-        round_w2(1, 1)
-        pick(1, 3, *first)
-        weave_z(1, *first)
+        product(0, 0, CHUNKS)
+        pick(1, 2, 0, LATE)
         quantize_w2(1, 0)
-        pick(1, 0, *second)
-        quantize_w2(1, 1)
-        pick(1, 1, *second)
-        quantize_z(1, *first)
-        product(1, *first)
-        pick(1, 2, *second)
-        pick(1, 3, *second)
-        weave_z(1, *second)
-        finish(0, *first)
+        pick(1, 3, 0, LATE)
+        weave_z(1, 0, LATE)
+        round_w2(1, 1)
+        quantize_w2(0, 1)
+        product(0, 1, CHUNKS)
         pick(1, 0, *third)
-        quantize_z(1, *second)
-        product(1, *second)
-        finish(1, *first)
-        for t in range(1, 4):
-            pick(1, t, *third)
+        pick(1, 1, *third)
+        quantize_z(1, 0, LATE)
+        product(1, 0, [first, second])
+        pick(1, 2, *third)
+        finish(nc.scalar.copy, 0, *first)
+        quantize_w2(1, 1)
+        product(1, 1, [first, second])
+        pick(1, 3, *third)
         weave_z(1, *third)
-        finish(0, *second)
-        finish(1, *second)
+        finish(nc.scalar.copy, 0, *second)
+        finish(nc.scalar.copy, 1, *first)
         quantize_z(1, *third)
-        product(1, *third)
+        for g in range(2):
+            product(1, g, [third])
+        finish(nc.scalar.copy, 1, *second)
         quantize_y(*first)
-        finish(0, *third)
-        finish(1, *third)
+        for g in range(2):
+            finish(nc.vector.tensor_copy, g, *third)
         quantize_y(*second)
         quantize_y(*third)
         for q in range(4):

@@ -19,9 +19,14 @@ MAX = mybir.AluOpType.max
 IDENTITY = mybir.ActivationFunctionType.Identity
 
 P = 128
+GROUP = 512
 BANK = 512
+PER_COLUMN = 16
+H_BANKS = 3
 LATE = 384
-CHUNKS = ((0, 256), (256, 128), (384, 128))
+PIECES = ((0, 256), (256, 128), (384, 128))
+XA_BUFS, XB_BUFS = 5, 2
+WA_AT, TAB_SC_AT, WB_AT, TAB1_AT = 0, 1024, 2048, 4096
 
 
 def tile_list_salmon_origin_features_kernel(
@@ -33,16 +38,16 @@ def tile_list_salmon_origin_features_kernel(
         lists = ctx.enter_context(tc.tile_pool(name="lists", bufs=1))
         sb = ctx.enter_context(tc.tile_pool(name="sb", bufs=1))
         shared = ctx.enter_context(tc.tile_pool(name="shared", bufs=1))
-        ring = ctx.enter_context(tc.tile_pool(name="ring", bufs=5))
+        ring = ctx.enter_context(tc.tile_pool(name="ring", bufs=XA_BUFS))
         psum = ctx.enter_context(tc.psum_pool(name="psum", bufs=1))
 
         def tile(shape, dtype, name, tag=None):
             return sb.tile(shape, dtype, name=name, tag=tag or name, align_bytes=64)
 
-        idx = lists.tile([P, S // 16], U16, name="idx")
-        idx2 = lists.tile([P, J // 16], U16, name="idx2")
-        idx3 = lists.tile([P, J // 16], U16, name="idx3")
-        tab_sc = shared.tile([P, T], U8, name="tab_sc", offset=1024)
+        idx = lists.tile([P, S // PER_COLUMN], U16, name="idx")
+        idx2 = lists.tile([P, J // PER_COLUMN], U16, name="idx2")
+        idx3 = lists.tile([P, J // PER_COLUMN], U16, name="idx3")
+        tab_sc = shared.tile([P, T], U8, name="tab_sc", offset=TAB_SC_AT)
         w1_sc_raw = tile([P, 2 * H], U8, "w1_sc_raw")
         v_sc = [tile([P, S], U8, "v_sc%d" % a) for a in range(2)]
         nc.vector.memset(w1_sc_raw[:].bitcast(I32), 0)
@@ -65,44 +70,48 @@ def tile_list_salmon_origin_features_kernel(
         nc.sync.dma_start(idx2[:], offs2)
         nc.sync.dma_start(idx3[:], offs3)
         load_table(0)
-        for q in range(4):
+        for quad in range(4):
             nc.scalar.dma_start(
-                out=w1_sc_raw[32 * q : 32 * q + 4, :].rearrange("r (a c) -> r a c", a=2).bitcast(I32),
-                in_=w1_scales[:, 4 * q : 4 * q + 4, :].rearrange("a r c -> r a c").bitcast(I32),
+                out=w1_sc_raw[32 * quad : 32 * quad + 4, :].rearrange("i (a c) -> i a c", a=2).bitcast(I32),
+                in_=w1_scales[:, 4 * quad : 4 * quad + 4, :].rearrange("a i c -> i a c").bitcast(I32),
             )
 
         picked_sc = tile([P, S], U8, "picked_sc")
         nc.vector.tensor_copy(picked_sc[:], tab_sc[:].indirect(idx[:]))
-        for a in range(2):
-            for q in range(4):
-                if (a, q) == (0, 1):
-                    tab.append(shared.tile([P, T], I32, name="tab1", offset=4096))
-                    load_table(1)
-                nc.sync.dma_start(
-                    out=v_sc[a][32 * q : 32 * q + 4, :].bitcast(I32),
-                    in_=picked_sc[16 * a + 4 * q : 16 * a + 4 * q + 4, :].bitcast(I32),
-                )
 
-        wa = shared.tile([P, J], F32, name="wa", offset=0)
-        wb = shared.tile([P, J], F32, name="wb", offset=2048)
+        def move_scale_rows(a, quad):
+            nc.sync.dma_start(
+                out=v_sc[a][32 * quad : 32 * quad + 4, :].bitcast(I32),
+                in_=picked_sc[16 * a + 4 * quad : 16 * a + 4 * quad + 4, :].bitcast(I32),
+            )
+
+        moves = [(a, quad) for a in range(2) for quad in range(4)]
+        move_scale_rows(*moves[0])
+        tab.append(shared.tile([P, T], I32, name="tab1", offset=TAB1_AT))
+        load_table(1)
+        for move in moves[1:]:
+            move_scale_rows(*move)
+
+        wa = shared.tile([P, J], F32, name="wa", offset=WA_AT)
+        wb = shared.tile([P, J], F32, name="wb", offset=WB_AT)
         nc.sync.dma_start(out=wa[:], in_=wga)
         nc.sync.dma_start(out=wb[:], in_=wgb)
 
         rows = {}
         for name, vec in (("b1", b1), ("d", d), ("b2", b2), ("rs", rs)):
             rows[name] = tile([P, 2, 4], F32, name + "_rows")
-            nc.gpsimd.dma_start(out=rows[name][:], in_=vec.rearrange("(b p t) -> p b t", b=2, t=4))
+            nc.gpsimd.dma_start(out=rows[name][:], in_=vec.rearrange("(g p t) -> p g t", g=2, t=4))
 
-        w1_q = [tile([P, 2 * 2 * 512], U8, "w1_q%d" % b) for b in range(2)]
-        w1_sc = [tile([P, 2 * 512], U8, "w1_sc%d" % b) for b in range(2)]
+        w1_q = [tile([P, 2 * 2 * GROUP], U8, "w1_q%d" % b) for b in range(2)]
+        w1_sc = [tile([P, 2 * GROUP], U8, "w1_sc%d" % b) for b in range(2)]
 
         def deal_w1(b):
-            words = w1_raw[:].bitcast(U16)[:, :, 512 * b : 512 * (b + 1)]
+            words = w1_raw[:].bitcast(U16)[:, :, GROUP * b : GROUP * (b + 1)]
             nc.vector.tensor_copy(
                 out=w1_q[b][:].bitcast(U16).rearrange("p (a t m) -> p a t m", a=2, t=4),
                 in_=words.rearrange("p a (m t) -> p a t m", t=4),
             )
-            scales = w1_sc_raw[:].rearrange("p (a c) -> p a c", a=2)[:, :, 512 * b : 512 * (b + 1)]
+            scales = w1_sc_raw[:].rearrange("p (a c) -> p a c", a=2)[:, :, GROUP * b : GROUP * (b + 1)]
             nc.vector.tensor_copy(
                 out=w1_sc[b][:].rearrange("p (a t m) -> p a t m", a=2, t=4),
                 in_=scales.rearrange("p a (m t) -> p a t m", t=4),
@@ -110,24 +119,25 @@ def tile_list_salmon_origin_features_kernel(
 
         deal_w1(0)
         v_q = {}
-        v_all = tile([P, S], U32, "v_q0")
-        nc.vector.tensor_copy(v_all[:], tab[0][:].bitcast(U32).indirect(idx[:]))
+        v_whole = tile([P, S], U32, "v_q0")
+        nc.vector.tensor_copy(v_whole[:], tab[0][:].bitcast(U32).indirect(idx[:]))
+        half_cols = BANK // PER_COLUMN
         for half in range(2):
-            v_q[0, half] = v_all[:, BANK * half : BANK * (half + 1)]
+            v_q[0, half] = v_whole[:, BANK * half : BANK * (half + 1)]
             v_half = tile([P, BANK], U32, "v_q1%d" % half)
             nc.vector.tensor_copy(
-                v_half[:], tab[1][:].bitcast(U32).indirect(idx[:, 32 * half : 32 * (half + 1)])
+                v_half[:], tab[1][:].bitcast(U32).indirect(idx[:, half_cols * half : half_cols * (half + 1)])
             )
             v_q[1, half] = v_half[:]
         deal_w1(1)
 
         w2_raw = [
             tile([P, 4, H], F32, "w2_raw0", tag="tab0"),
-            shared.tile([P, 4, H], F32, name="w2_raw1", offset=4096),
+            shared.tile([P, 4, H], F32, name="w2_raw1", offset=TAB1_AT),
         ]
         for b in range(2):
             nc.sync.dma_start(
-                out=w2_raw[b][:], in_=w2[512 * b : 512 * (b + 1), :].rearrange("(p j) n -> p j n", j=4)
+                out=w2_raw[b][:], in_=w2[GROUP * b : GROUP * (b + 1), :].rearrange("(p j) n -> p j n", j=4)
             )
 
         h = {}
@@ -135,9 +145,10 @@ def tile_list_salmon_origin_features_kernel(
             for t in range(4):
                 h[b, t] = tile([P, S], F32, "h%d%d" % (b, t))
                 for half in range(2):
-                    acc = psum.tile([P, BANK], F32, name="acc", tag="bank%d" % ((2 * (4 * b + t) + half) % 3))
+                    turn = 2 * (4 * b + t) + half
+                    acc = psum.tile([P, BANK], F32, name="acc", tag="bank%d" % (turn % H_BANKS))
                     for a in range(2):
-                        col = 512 * a + P * t
+                        col = GROUP * a + P * t
                         nc.tensor.matmul_mx(
                             out=acc[:],
                             lhsT=w1_q[b][:, 2 * col : 2 * (col + P)].bitcast(FP4X4),
@@ -156,34 +167,38 @@ def tile_list_salmon_origin_features_kernel(
         w2_bf, w2_q, w2_sc = {}, {}, {}
         z, z_bf, z_q, z_sc = {}, {}, {}, {}
         side, y, y_bf, y_q, banks = {}, {}, {}, {}, {}
-        chain = ["xb"]
+
+        def run_start(group, j0):
+            return 0 if group == 0 or j0 < LATE else LATE
 
         def round_w2(b, g):
-            w2_bf[b, g] = tile([P, 4 * 512], BF16, "w2_bf%d%d" % (b, g))
+            w2_bf[b, g] = tile([P, 4 * GROUP], BF16, "w2_bf%d%d" % (b, g))
             nc.scalar.copy(
                 out=w2_bf[b, g][:].rearrange("p (t m j) -> p m t j", t=4, j=4),
-                in_=w2_raw[b][:, :, 512 * g : 512 * (g + 1)].rearrange("p j (m t) -> p m t j", t=4),
+                in_=w2_raw[b][:, :, GROUP * g : GROUP * (g + 1)].rearrange("p j (m t) -> p m t j", t=4),
             )
 
         def quantize_w2(b, g):
-            w2_q[b, g] = tile([P, 512], U32, "w2_q%d%d" % (b, g))
-            w2_sc[b, g] = tile([P, 512], U8, "w2_sc%d%d" % (b, g))
+            w2_q[b, g] = tile([P, GROUP], U32, "w2_q%d%d" % (b, g))
+            w2_sc[b, g] = tile([P, GROUP], U8, "w2_sc%d%d" % (b, g))
             nc.vector.quantize_mx(out=w2_q[b, g][:].bitcast(FP8X4), scales=w2_sc[b, g][:], in_=w2_bf[b, g][:])
-            chain[0] = "w2_bf%d%d" % (b, g)
 
-        def interleave(copy, dst, src):
+        def weave(copy, dst, src):
             copy(
                 out=dst.rearrange("p (c i t) -> p c t i", i=4, t=4),
                 in_=src.rearrange("p t (c i) -> p c t i", i=4),
             )
 
-        def pick(b, t, j0, w):
+        def pick(b, t, j0, w, after=None):
             if t == 0:
                 z[b, j0] = tile([P, 4, w], BF16, "z%d_%d" % (b, j0))
                 side[b, j0] = tile([P, 4, w], F32, "side%d_%d" % (b, j0))
-            cols = slice(j0 // 16, (j0 + w) // 16)
+            cols = slice(j0 // PER_COLUMN, (j0 + w) // PER_COLUMN)
             xa = ring.tile([P, w], F32, name="xa", tag="xa")
-            xb = tile([P, w], F32, "xb", tag=chain[0])
+            if after is None:
+                xb = ring.tile([P, w], F32, name="xb", tag="xb", bufs=XB_BUFS)
+            else:
+                xb = tile([P, w], F32, "xb_late", tag=after)
             nc.vector.tensor_tensor(xa[:], h[b, t][:].indirect(idx2[:, cols]), wa[:, j0 : j0 + w], MULT)
             nc.vector.tensor_tensor(xb[:], h[b, t][:].indirect(idx3[:, cols]), wb[:, j0 : j0 + w], MULT)
             nc.vector.scalar_tensor_tensor(
@@ -196,18 +211,17 @@ def tile_list_salmon_origin_features_kernel(
 
         def weave_z(b, j0, w):
             z_bf[b, j0] = tile([P, 4 * w], BF16, "z_bf%d_%d" % (b, j0))
-            interleave(nc.scalar.copy, z_bf[b, j0][:], z[b, j0][:])
+            weave(nc.scalar.copy, z_bf[b, j0][:], z[b, j0][:])
 
         def quantize_z(b, j0, w):
             z_q[b, j0] = tile([P, w], U32, "z_q%d_%d" % (b, j0))
             z_sc[b, j0] = tile([P, w], U8, "z_sc%d_%d" % (b, j0))
             nc.vector.quantize_mx(out=z_q[b, j0][:].bitcast(FP8X4), scales=z_sc[b, j0][:], in_=z_bf[b, j0][:])
-            chain[0] = "z_bf%d_%d" % (b, j0)
 
-        def product(b, g, chunks):
-            for j0, w in chunks:
+        def product(b, g, pieces):
+            for j0, w in pieces:
                 per_bank = BANK // w
-                z0 = 0 if b == 0 or j0 < LATE else LATE
+                z0 = run_start(b, j0)
                 for t in range(4):
                     key = (j0, g, t // per_bank)
                     slot = t % per_bank
@@ -225,7 +239,7 @@ def tile_list_salmon_origin_features_kernel(
 
         def finish(copy, g, j0, w):
             per_bank = BANK // w
-            z0 = 0 if g == 0 or j0 < LATE else LATE
+            z0 = run_start(g, j0)
             y[g, j0] = tile([P, 4, w], F32, "y%d_%d" % (g, j0))
             for n in range(4 // per_bank):
                 ts = slice(n * per_bank, (n + 1) * per_bank)
@@ -236,11 +250,11 @@ def tile_list_salmon_origin_features_kernel(
                     ADD,
                 )
             nc.sync.dma_start(
-                out=out_0[512 * g : 512 * (g + 1), j0 : j0 + w].rearrange("(p t) j -> p t j", t=4),
+                out=out_0[GROUP * g : GROUP * (g + 1), j0 : j0 + w].rearrange("(p t) j -> p t j", t=4),
                 in_=y[g, j0][:],
             )
             y_bf[g, j0] = tile([P, 4 * w], BF16, "y_bf%d_%d" % (g, j0))
-            interleave(copy, y_bf[g, j0][:], y[g, j0][:])
+            weave(copy, y_bf[g, j0][:], y[g, j0][:])
 
         def quantize_y(j0, w):
             y_q[j0] = tile([P, 2, w], I32, "y_q%d" % j0)
@@ -253,7 +267,7 @@ def tile_list_salmon_origin_features_kernel(
                 in_=y_q[j0][:],
             )
 
-        first, second, third = CHUNKS
+        first, second, third = PIECES
         for t in range(3):
             pick(0, t, 0, J)
         round_w2(0, 0)
@@ -265,23 +279,23 @@ def tile_list_salmon_origin_features_kernel(
         pick(1, 1, 0, LATE)
         round_w2(0, 1)
         quantize_z(0, 0, J)
-        product(0, 0, CHUNKS)
+        product(0, 0, PIECES)
         pick(1, 2, 0, LATE)
-        quantize_w2(1, 0)
-        pick(1, 3, 0, LATE)
+        pick(1, 3, 0, LATE, after="z_bf0_0")
         weave_z(1, 0, LATE)
         round_w2(1, 1)
+        quantize_w2(1, 0)
+        pick(1, 0, *third, after="w2_bf10")
         quantize_w2(0, 1)
-        product(0, 1, CHUNKS)
-        pick(1, 0, *third)
-        pick(1, 1, *third)
+        product(0, 1, PIECES)
+        pick(1, 1, *third, after="w2_bf01")
         quantize_z(1, 0, LATE)
         product(1, 0, [first, second])
-        pick(1, 2, *third)
+        pick(1, 2, *third, after="z_bf1_0")
         finish(nc.scalar.copy, 0, *first)
         quantize_w2(1, 1)
         product(1, 1, [first, second])
-        pick(1, 3, *third)
+        pick(1, 3, *third, after="w2_bf11")
         weave_z(1, *third)
         finish(nc.scalar.copy, 0, *second)
         finish(nc.scalar.copy, 1, *first)
@@ -294,9 +308,9 @@ def tile_list_salmon_origin_features_kernel(
             finish(nc.vector.tensor_copy, g, *third)
         quantize_y(*second)
         quantize_y(*third)
-        for q in range(4):
-            queue = nc.sync if q % 2 == 0 else nc.scalar
+        for quad in range(4):
+            queue = nc.sync if quad % 2 == 0 else nc.scalar
             queue.dma_start(
-                out=out_2[:, 4 * q : 4 * q + 4, :].rearrange("g r m -> r g m").bitcast(I32),
-                in_=y_sc[32 * q : 32 * q + 4, :, :].bitcast(I32),
+                out=out_2[:, 4 * quad : 4 * quad + 4, :].rearrange("g i m -> i g m").bitcast(I32),
+                in_=y_sc[32 * quad : 32 * quad + 4, :, :].bitcast(I32),
             )

from contextlib import ExitStack

import concourse.mybir as mybir

K, H, T, S, J = 1024, 1024, 4096, 1024, 512
FLOPS = 2 * K * H * S + 2 * H * H * J

F32 = mybir.dt.float32
BF16 = mybir.dt.bfloat16
I32 = mybir.dt.int32
U32 = mybir.dt.uint32
U16 = mybir.dt.uint16
U8 = mybir.dt.uint8
FP8X4 = mybir.dt.float8_e4m3fn_x4
FP4X4 = mybir.dt.float4_e2m1fn_x4
MULT = mybir.AluOpType.mult
ADD = mybir.AluOpType.add
MAX = mybir.AluOpType.max
IDENTITY = mybir.ActivationFunctionType.Identity

P = 128
GROUP = 512
BANK = 512
PER_COLUMN = 16
H_BANKS = 3
LATE = 384
PIECES = ((0, 256), (256, 128), (384, 128))
XA_BUFS, XB_BUFS = 5, 2
WA_AT, TAB_SC_AT, WB_AT, TAB1_AT = 0, 1024, 2048, 4096


def tile_list_salmon_origin_features_kernel(
    tc, tab_words, tab_scales, offs, w1_words, w1_scales, b1, offs2, offs3, wga, wgb, d, w2, b2, rs,
    out_0, out_1, out_2,
):
    nc = tc.nc
    with ExitStack() as ctx:
        lists = ctx.enter_context(tc.tile_pool(name="lists", bufs=1))
        sb = ctx.enter_context(tc.tile_pool(name="sb", bufs=1))
        shared = ctx.enter_context(tc.tile_pool(name="shared", bufs=1))
        ring = ctx.enter_context(tc.tile_pool(name="ring", bufs=XA_BUFS))
        psum = ctx.enter_context(tc.psum_pool(name="psum", bufs=1))

        def tile(shape, dtype, name, tag=None):
            return sb.tile(shape, dtype, name=name, tag=tag or name, align_bytes=64)

        idx = lists.tile([P, S // PER_COLUMN], U16, name="idx")
        idx2 = lists.tile([P, J // PER_COLUMN], U16, name="idx2")
        idx3 = lists.tile([P, J // PER_COLUMN], U16, name="idx3")
        tab_sc = shared.tile([P, T], U8, name="tab_sc", offset=TAB_SC_AT)
        w1_sc_raw = tile([P, 2 * H], U8, "w1_sc_raw")
        v_sc = [tile([P, S], U8, "v_sc%d" % a) for a in range(2)]
        nc.vector.memset(w1_sc_raw[:].bitcast(I32), 0)
        nc.vector.memset(tab_sc[32:64, :].bitcast(I32), 0)
        nc.vector.memset(tab_sc[64:128, :].bitcast(I32), 0)
        for a in range(2):
            nc.vector.memset(v_sc[a][:].bitcast(I32), 0)

        w1_raw = tile([P, 2, 2 * H], U8, "w1_raw")
        tab = [tile([P, T], I32, "tab0")]

        def load_table(a):
            nc.sync.dma_start(out=tab[a][:], in_=tab_words[a].rearrange("p t i -> p (t i)").bitcast(I32))

        nc.sync.dma_start(idx[:], offs)
        nc.sync.dma_start(
            out=tab_sc[0:32, :].bitcast(I32), in_=tab_scales.rearrange("a q t -> (a q) t").bitcast(I32)
        )
        nc.sync.dma_start(out=w1_raw[:].bitcast(I32), in_=w1_words.rearrange("a p c -> p a c").bitcast(I32))
        nc.sync.dma_start(idx2[:], offs2)
        nc.sync.dma_start(idx3[:], offs3)
        load_table(0)
        for quad in range(4):
            nc.scalar.dma_start(
                out=w1_sc_raw[32 * quad : 32 * quad + 4, :].rearrange("i (a c) -> i a c", a=2).bitcast(I32),
                in_=w1_scales[:, 4 * quad : 4 * quad + 4, :].rearrange("a i c -> i a c").bitcast(I32),
            )

        picked_sc = tile([P, S], U8, "picked_sc")
        nc.vector.tensor_copy(picked_sc[:], tab_sc[:].indirect(idx[:]))

        def move_scale_rows(a, quad):
            nc.sync.dma_start(
                out=v_sc[a][32 * quad : 32 * quad + 4, :].bitcast(I32),
                in_=picked_sc[16 * a + 4 * quad : 16 * a + 4 * quad + 4, :].bitcast(I32),
            )

        moves = [(a, quad) for a in range(2) for quad in range(4)]
        move_scale_rows(*moves[0])
        tab.append(shared.tile([P, T], I32, name="tab1", offset=TAB1_AT))
        load_table(1)
        for move in moves[1:]:
            move_scale_rows(*move)

        wa = shared.tile([P, J], F32, name="wa", offset=WA_AT)
        wb = shared.tile([P, J], F32, name="wb", offset=WB_AT)
        nc.sync.dma_start(out=wa[:], in_=wga)
        nc.sync.dma_start(out=wb[:], in_=wgb)

        rows = {}
        for name, vec in (("b1", b1), ("d", d), ("b2", b2), ("rs", rs)):
            rows[name] = tile([P, 2, 4], F32, name + "_rows")
            nc.gpsimd.dma_start(out=rows[name][:], in_=vec.rearrange("(g p t) -> p g t", g=2, t=4))

        w1_q = [tile([P, 2 * 2 * GROUP], U8, "w1_q%d" % b) for b in range(2)]
        w1_sc = [tile([P, 2 * GROUP], U8, "w1_sc%d" % b) for b in range(2)]

        def deal_w1(b):
            words = w1_raw[:].bitcast(U16)[:, :, GROUP * b : GROUP * (b + 1)]
            nc.vector.tensor_copy(
                out=w1_q[b][:].bitcast(U16).rearrange("p (a t m) -> p a t m", a=2, t=4),
                in_=words.rearrange("p a (m t) -> p a t m", t=4),
            )
            scales = w1_sc_raw[:].rearrange("p (a c) -> p a c", a=2)[:, :, GROUP * b : GROUP * (b + 1)]
            nc.vector.tensor_copy(
                out=w1_sc[b][:].rearrange("p (a t m) -> p a t m", a=2, t=4),
                in_=scales.rearrange("p a (m t) -> p a t m", t=4),
            )

        deal_w1(0)
        v_q = {}
        v_whole = tile([P, S], U32, "v_q0")
        nc.vector.tensor_copy(v_whole[:], tab[0][:].bitcast(U32).indirect(idx[:]))
        half_cols = BANK // PER_COLUMN
        for half in range(2):
            v_q[0, half] = v_whole[:, BANK * half : BANK * (half + 1)]
            v_half = tile([P, BANK], U32, "v_q1%d" % half)
            nc.vector.tensor_copy(
                v_half[:], tab[1][:].bitcast(U32).indirect(idx[:, half_cols * half : half_cols * (half + 1)])
            )
            v_q[1, half] = v_half[:]
        deal_w1(1)

        w2_raw = [
            tile([P, 4, H], F32, "w2_raw0", tag="tab0"),
            shared.tile([P, 4, H], F32, name="w2_raw1", offset=TAB1_AT),
        ]
        for b in range(2):
            nc.sync.dma_start(
                out=w2_raw[b][:], in_=w2[GROUP * b : GROUP * (b + 1), :].rearrange("(p j) n -> p j n", j=4)
            )

        h = {}
        for b in range(2):
            for t in range(4):
                h[b, t] = tile([P, S], F32, "h%d%d" % (b, t))
                for half in range(2):
                    turn = 2 * (4 * b + t) + half
                    acc = psum.tile([P, BANK], F32, name="acc", tag="bank%d" % (turn % H_BANKS))
                    for a in range(2):
                        col = GROUP * a + P * t
                        nc.tensor.matmul_mx(
                            out=acc[:],
                            lhsT=w1_q[b][:, 2 * col : 2 * (col + P)].bitcast(FP4X4),
                            lhsT_scale=w1_sc[b][:, col : col + P],
                            rhs=v_q[a, half].bitcast(FP8X4),
                            rhs_scale=v_sc[a][:, BANK * half : BANK * (half + 1)],
                            start=(a == 0),
                            stop=(a == 1),
                        )
                    nc.scalar.activation(
                        out=h[b, t][:, BANK * half : BANK * (half + 1)], in_=acc[:], func=IDENTITY,
                        bias=rows["b1"][:, b, t : t + 1],
                    )

        y_sc = tile([P, 2, J], U8, "y_sc")
        w2_bf, w2_q, w2_sc = {}, {}, {}
        z, z_bf, z_q, z_sc = {}, {}, {}, {}
        side, y, y_bf, y_q, banks = {}, {}, {}, {}, {}

        def run_start(group, j0):
            return 0 if group == 0 or j0 < LATE else LATE

        def round_w2(b, g):
            w2_bf[b, g] = tile([P, 4 * GROUP], BF16, "w2_bf%d%d" % (b, g))
            nc.scalar.copy(
                out=w2_bf[b, g][:].rearrange("p (t m j) -> p m t j", t=4, j=4),
                in_=w2_raw[b][:, :, GROUP * g : GROUP * (g + 1)].rearrange("p j (m t) -> p m t j", t=4),
            )

        def quantize_w2(b, g):
            w2_q[b, g] = tile([P, GROUP], U32, "w2_q%d%d" % (b, g))
            w2_sc[b, g] = tile([P, GROUP], U8, "w2_sc%d%d" % (b, g))
            nc.vector.quantize_mx(out=w2_q[b, g][:].bitcast(FP8X4), scales=w2_sc[b, g][:], in_=w2_bf[b, g][:])

        def weave(copy, dst, src):
            copy(
                out=dst.rearrange("p (c i t) -> p c t i", i=4, t=4),
                in_=src.rearrange("p t (c i) -> p c t i", i=4),
            )

        def pick(b, t, j0, w, after=None):
            if t == 0:
                z[b, j0] = tile([P, 4, w], BF16, "z%d_%d" % (b, j0))
                side[b, j0] = tile([P, 4, w], F32, "side%d_%d" % (b, j0))
            cols = slice(j0 // PER_COLUMN, (j0 + w) // PER_COLUMN)
            xa = ring.tile([P, w], F32, name="xa", tag="xa")
            if after is None:
                xb = ring.tile([P, w], F32, name="xb", tag="xb", bufs=XB_BUFS)
            else:
                xb = tile([P, w], F32, "xb_late", tag=after)
            nc.vector.tensor_tensor(xa[:], h[b, t][:].indirect(idx2[:, cols]), wa[:, j0 : j0 + w], MULT)
            nc.vector.tensor_tensor(xb[:], h[b, t][:].indirect(idx3[:, cols]), wb[:, j0 : j0 + w], MULT)
            nc.vector.scalar_tensor_tensor(
                out=z[b, j0][:, t, :], in0=xb[:], scalar=rows["d"][:, b, t : t + 1], in1=xa[:], op0=ADD, op1=MAX
            )
            nc.scalar.activation(
                out=side[b, j0][:, t, :], in_=xa[:], func=IDENTITY,
                scale=rows["rs"][:, b, t : t + 1], bias=rows["b2"][:, b, t : t + 1],
            )

        def weave_z(b, j0, w):
            z_bf[b, j0] = tile([P, 4 * w], BF16, "z_bf%d_%d" % (b, j0))
            weave(nc.scalar.copy, z_bf[b, j0][:], z[b, j0][:])

        def quantize_z(b, j0, w):
            z_q[b, j0] = tile([P, w], U32, "z_q%d_%d" % (b, j0))
            z_sc[b, j0] = tile([P, w], U8, "z_sc%d_%d" % (b, j0))
            nc.vector.quantize_mx(out=z_q[b, j0][:].bitcast(FP8X4), scales=z_sc[b, j0][:], in_=z_bf[b, j0][:])

        def product(b, g, pieces):
            for j0, w in pieces:
                per_bank = BANK // w
                z0 = run_start(b, j0)
                for t in range(4):
                    key = (j0, g, t // per_bank)
                    slot = t % per_bank
                    if b == 0 and slot == 0:
                        banks[key] = psum.tile([P, BANK], F32, name="acc", tag="bank%d" % len(banks))
                    nc.tensor.matmul_mx(
                        out=banks[key][:, slot * w : (slot + 1) * w],
                        lhsT=w2_q[b, g][:, P * t : P * (t + 1)].bitcast(FP8X4),
                        lhsT_scale=w2_sc[b, g][:, P * t : P * (t + 1)],
                        rhs=z_q[b, z0][:, j0 - z0 : j0 - z0 + w].bitcast(FP8X4),
                        rhs_scale=z_sc[b, z0][:, j0 - z0 : j0 - z0 + w],
                        start=(b == 0 and slot == 0),
                        stop=(b == 1 and slot == per_bank - 1),
                    )

        def finish(copy, g, j0, w):
            per_bank = BANK // w
            z0 = run_start(g, j0)
            y[g, j0] = tile([P, 4, w], F32, "y%d_%d" % (g, j0))
            for n in range(4 // per_bank):
                ts = slice(n * per_bank, (n + 1) * per_bank)
                nc.vector.tensor_tensor(
                    y[g, j0][:, ts, :],
                    banks[j0, g, n][:].rearrange("p (t j) -> p t j", j=w),
                    side[g, z0][:, ts, j0 - z0 : j0 - z0 + w],
                    ADD,
                )
            nc.sync.dma_start(
                out=out_0[GROUP * g : GROUP * (g + 1), j0 : j0 + w].rearrange("(p t) j -> p t j", t=4),
                in_=y[g, j0][:],
            )
            y_bf[g, j0] = tile([P, 4 * w], BF16, "y_bf%d_%d" % (g, j0))
            weave(copy, y_bf[g, j0][:], y[g, j0][:])

        def quantize_y(j0, w):
            y_q[j0] = tile([P, 2, w], I32, "y_q%d" % j0)
            for g in range(2):
                nc.vector.quantize_mx(
                    out=y_q[j0][:, g, :].bitcast(FP8X4), scales=y_sc[:, g, j0 : j0 + w], in_=y_bf[g, j0][:]
                )
            nc.sync.dma_start(
                out=out_1.rearrange("g p m t -> p g (m t)")[:, :, 4 * j0 : 4 * (j0 + w)].bitcast(I32),
                in_=y_q[j0][:],
            )

        first, second, third = PIECES
        for t in range(3):
            pick(0, t, 0, J)
        round_w2(0, 0)
        pick(0, 3, 0, J)
        weave_z(0, 0, J)
        round_w2(1, 0)
        pick(1, 0, 0, LATE)
        quantize_w2(0, 0)
        pick(1, 1, 0, LATE)
        round_w2(0, 1)
        quantize_z(0, 0, J)
        product(0, 0, PIECES)
        pick(1, 2, 0, LATE)
        pick(1, 3, 0, LATE, after="z_bf0_0")
        weave_z(1, 0, LATE)
        round_w2(1, 1)
        quantize_w2(1, 0)
        pick(1, 0, *third, after="w2_bf10")
        quantize_w2(0, 1)
        product(0, 1, PIECES)
        pick(1, 1, *third, after="w2_bf01")
        quantize_z(1, 0, LATE)
        product(1, 0, [first, second])
        pick(1, 2, *third, after="z_bf1_0")
        finish(nc.scalar.copy, 0, *first)
        quantize_w2(1, 1)
        product(1, 1, [first, second])
        pick(1, 3, *third, after="w2_bf11")
        weave_z(1, *third)
        finish(nc.scalar.copy, 0, *second)
        finish(nc.scalar.copy, 1, *first)
        quantize_z(1, *third)
        for g in range(2):
            product(1, g, [third])
        finish(nc.scalar.copy, 1, *second)
        quantize_y(*first)
        for g in range(2):
            finish(nc.vector.tensor_copy, g, *third)
        quantize_y(*second)
        quantize_y(*third)
        for quad in range(4):
            queue = nc.sync if quad % 2 == 0 else nc.scalar
            queue.dma_start(
                out=out_2[:, 4 * quad : 4 * quad + 4, :].rearrange("g i m -> i g m").bitcast(I32),
                in_=y_sc[32 * quad : 32 * quad + 4, :, :].bitcast(I32),
            )
